import numpy as np
import ml_dtypes


def mxq(x, axis, fmt="e4m3"):
    dtype, down = {"e4m3": (ml_dtypes.float8_e4m3fn, 7), "e5m2": (ml_dtypes.float8_e5m2, 14)}[fmt]
    v = np.moveaxis(np.asarray(x, np.float32).astype(ml_dtypes.bfloat16).astype(np.float64), axis, -1)
    blocks = v.reshape(v.shape[:-1] + (-1, 32))
    amax = np.abs(blocks).max(-1, keepdims=True)
    byte = np.maximum(np.where(amax > 0, np.frexp(amax)[1] - 1 + 127, 0) - down, 1)
    scale = np.exp2(byte - 127.0)
    codes = (blocks / scale).astype(np.float32).astype(dtype).astype(np.float64)
    return np.moveaxis((codes * scale).reshape(v.shape), -1, axis)


WIDE = False


def mx_kscale(k):
    if not WIDE:
        return np.ones(k)
    levels = np.array([10, -10, 5, -5, 0])
    if k % 512:
        return np.exp2(np.random.permutation(np.resize(levels, k // 32))).repeat(32)
    a = np.empty((k // 512, 16))
    for p in range(k // 512):
        a[p, :8] = np.random.permutation(np.resize(levels, 8))
        for g in range(8):
            far = levels[np.abs(levels - a[p, g]) >= 10]
            a[p, g + 8] = far[np.random.randint(len(far))]
    return np.exp2(a.ravel()).repeat(32)


def f64(x):
    return np.asarray(x).astype(np.float64)


def striped(idx):
    return np.tile(idx.reshape(-1, 16).T, (8, 1)).astype(np.uint16)


def unstriped(offs):
    return offs[:16].T.reshape(-1).astype(np.int64)


def striped8(idx):
    return np.concatenate([x.reshape(-1, 16).T for x in idx]).astype(np.uint16)


def runs(offs, k):
    lists = np.stack([offs[16 * r : 16 * r + 16].T.reshape(-1) for r in range(8)]).astype(np.int64)
    return lists[np.arange(k) % 512 // 64]


def pack_weight(w):
    k, n = w.shape
    w = f64(np.asarray(w, np.float32).astype(ml_dtypes.bfloat16)).reshape(k // 32, 32, n)
    amax = np.abs(w).max(1)
    byte = np.clip(np.where(amax > 0, np.frexp(amax)[1] - 1 + 127 - 7, 1), 1, 254)
    scaled = (w * np.exp2(127.0 - byte)[:, None, :]).reshape(k, n).astype(np.float32)
    words = np.ascontiguousarray(scaled.reshape(k // 512, 128, 4, n).transpose(0, 1, 3, 2)).astype(ml_dtypes.float8_e4m3fn).view(np.uint8)
    return words, np.ascontiguousarray(byte.astype(np.uint8).reshape(k // 512, 16, n))


def unpack_weight(words, scales):
    g, p, n, _ = words.shape
    vals = np.ascontiguousarray(words).view(ml_dtypes.float8_e4m3fn).astype(np.float64) * np.repeat(np.exp2(scales.astype(np.float64) - 127.0), 8, axis=1)[..., None]
    return vals.transpose(0, 1, 3, 2).reshape(g * 512, n)


E2M1 = np.array([0.0, 0.5, 1.0, 1.5, 2.0, 3.0, 4.0, 6.0, -0.0, -0.5, -1.0, -1.5, -2.0, -3.0, -4.0, -6.0])


def pack_fp4(w):
    k, n = w.shape
    w = f64(np.asarray(w, np.float32).astype(ml_dtypes.bfloat16)).reshape(k // 32, 32, n)
    amax = np.abs(w).max(1)
    mant, ex = np.frexp(amax / 6.0)
    byte = np.clip(np.where(amax > 0, np.where(mant > 0.5, ex, ex - 1) + 127, 1), 1, 254)
    scaled = (w * np.exp2(127.0 - byte)[:, None, :]).reshape(k, n).astype(np.float32)
    c = np.ascontiguousarray(scaled.reshape(k // 512, 128, 4, n).transpose(0, 1, 3, 2)).astype(ml_dtypes.float4_e2m1fn).view(np.uint8) & 0xF
    words = (c[..., 0::2] | (c[..., 1::2] << 4)).reshape(k // 512, 128, 2 * n)
    return np.ascontiguousarray(words), np.ascontiguousarray(byte.astype(np.uint8).reshape(k // 512, 16, n))


def unpack_fp4(words, scales):
    g, _, n = scales.shape
    words = np.ascontiguousarray(words).reshape(g, 128, n, 2)
    nib = np.empty((g, 128, n, 4), np.uint8)
    nib[..., 0::2] = words & 0xF
    nib[..., 1::2] = words >> 4
    vals = E2M1[nib] * np.repeat(np.exp2(scales.astype(np.float64) - 127.0), 8, axis=1)[..., None]
    return vals.transpose(0, 1, 3, 2).reshape(g * 512, n)


def sigmoid(v):
    return 1.0 / (1.0 + np.exp(-np.maximum(v, -700.0)))

def planes(y):
    n, m = y.shape
    v = y.astype(np.float32).astype(ml_dtypes.bfloat16).astype(np.float64).reshape(n // 32, 32, m)
    top = np.abs(v).max(1)
    byte = np.clip(np.where(top > 0, np.frexp(top)[1] - 1 + 127 - 7, 1), 1, 254)
    codes = (v * np.exp2(127.0 - byte)[:, None, :]).reshape(n, m).astype(np.float32).astype(ml_dtypes.float8_e4m3fn).view(np.uint8)
    words = codes.reshape(n // 512, 128, 4, m).transpose(0, 1, 3, 2)
    return np.ascontiguousarray(words), np.ascontiguousarray(byte.astype(np.uint8).reshape(n // 512, 16, m))


K, T, S, H, W = 512, 2048, 512, 512, 256


def setup_inputs():
    n = np.random.standard_normal
    s = mx_kscale(K)[:, None]
    u = mx_kscale(S)
    packed_xT = pack_weight(n((K, T)) * s)
    packed_w1 = pack_fp4(n((K, H)) / np.sqrt(K) / s)
    perm = np.stack([np.random.permutation(S) for _ in range(8)])
    return {
        "x_words": packed_xT[0],
        "x_scales": packed_xT[1],
        "w1_words": packed_w1[0],
        "w1_scales": packed_w1[1],
        "ga": (np.random.uniform(0.5, 1.5, (H, 1)) * u[:, None]).astype(np.float32),
        "gb": (np.random.uniform(0.5, 1.5, (H, 1)) / u[:, None]).astype(np.float32),
        "offs": striped(np.random.permutation(T)[:S]),
        "n1": striped8(perm[:, :W]),
        "n2": striped8(perm[:, W:]),
        "n3": striped8(np.stack([np.random.permutation(S) for _ in range(8)])),
        "n4": striped8(np.stack([np.random.permutation(S) for _ in range(8)])),
        "n5": striped8(np.stack([np.random.permutation(S) for _ in range(8)])),
        "n6": striped8(np.stack([np.random.permutation(S) for _ in range(8)])),
        "n7": striped8(np.stack([np.random.permutation(S) for _ in range(8)])),
        "n8": striped8(np.stack([np.random.permutation(S) for _ in range(8)])),
        "n9": striped8(np.stack([np.random.permutation(S) for _ in range(8)])),
    }


def reference(x_words, x_scales, w1_words, w1_scales, ga, gb, offs, n1, n2, n3, n4, n5, n6, n7, n8, n9):
    xq = unpack_weight(x_words, x_scales)[:, unstriped(offs)]
    y = unpack_fp4(w1_words, w1_scales).T @ xq
    pa = y[np.arange(H)[:, None], runs(n1, H)]
    pb = y[np.arange(H)[:, None], runs(n2, H)]
    rb = np.maximum(pa, pb)
    ra = pa / (np.abs(pb) + 0.5)
    ds = np.zeros((H, S))
    ds[np.arange(H)[:, None], runs(n1, H)] = ra
    dt = ds.copy()
    dt[np.arange(H)[:, None], runs(n2, H)] = rb
    z = f64(ga) * dt
    z2 = f64(gb) * (0.75 * ((y[np.arange(H)[:, None], runs(n3, H)]) * (y[np.arange(H)[:, None], runs(n4, H)]) - ((y[np.arange(H)[:, None], runs(n5, H)]) * (y[np.arange(H)[:, None], runs(n6, H)]))))
    s = 0.0625 * ((mxq(z, 0, "e4m3").T @ mxq(z2, 0, "e4m3")))
    pa2 = s[np.arange(S)[:, None], runs(n7, S)]
    out_0 = pa2 + (sigmoid(s[np.arange(S)[:, None], runs(n8, S)])) * (s[np.arange(S)[:, None], runs(n9, S)] - pa2)
    return (out_0,) + planes(out_0)

@@ -1,0 +1,226 @@
+from contextlib import ExitStack
+
+import concourse.mybir as mybir
+
+F32 = mybir.dt.float32
+BF16 = mybir.dt.bfloat16
+I32 = mybir.dt.int32
+U32 = mybir.dt.uint32
+U16 = mybir.dt.uint16
+U8 = mybir.dt.uint8
+FP8X4 = mybir.dt.float8_e4m3fn_x4
+FP4X4 = mybir.dt.float4_e2m1fn_x4
+ALU = mybir.AluOpType
+ACT = mybir.ActivationFunctionType
+
+P = 128
+PACK = 4
+T = 2048
+S = 512
+W = 256
+FLOPS = 2 * 2 * 512 * 512 * 512
+
+Z2_CHUNKS = ((0, 256), (256, 128), (384, 128))
+OUT_CHUNKS = ((0, 256), (256, 128), (384, 128))
+
+
+def entries(list_tile, start, count):
+    return list_tile[:, start // 16 : (start + count) // 16]
+
+
+def four_lines(ap_tc):
+    return ap_tc.rearrange("p t (c i) -> p c t i", i=4)
+
+
+def four_lines_packed(ap_ct):
+    return ap_ct.rearrange("p (c i) t -> p c t i", i=4)
+
+
+def tile_picked_selfratiodetlerp_none_po_kernel(
+    tc, x_words, x_scales, w1_words, w1_scales, ga, gb, offs, n1, n2, n3, n4, n5, n6, n7, n8, n9, out_0, out_1, out_2
+):
+    nc = tc.nc
+    with ExitStack() as ctx:
+        lists = ctx.enter_context(tc.tile_pool(name="lists", bufs=1))
+        keep = ctx.enter_context(tc.tile_pool(name="keep", bufs=1))
+        psum = ctx.enter_context(tc.psum_pool(name="psum", bufs=1))
+
+        def load_list(name, src):
+            tile = lists.tile([P, src.shape[1]], U16, name=name)
+            nc.sync.dma_start(tile[:], src)
+            return tile
+
+        def load_scale_rows(queue, tile, src):
+            for q in range(4):
+                rows = src[0, 4 * q : 4 * q + 4, :].bitcast(I32)
+                queue.dma_start(tile[32 * q : 32 * q + 32, :].bitcast(I32), rows.partition_broadcast(8))
+
+        x_sc = keep.tile([P, T], U8, align_bytes=64)
+        w_sc = keep.tile([P, S], U8, align_bytes=64)
+
+        x_wd = keep.tile([P, T], I32, align_bytes=64)
+        w_wd = keep.tile([P, 2 * S], U8, align_bytes=64)
+        offs_sb = load_list("offs_sb", offs)
+        load_scale_rows(nc.sync, x_sc, x_scales)
+        nc.sync.dma_start(w_wd[:].bitcast(I32), w1_words[0].bitcast(I32))
+        nc.sync.dma_start(x_wd[:], x_words[0].rearrange("p n t -> p (n t)").bitcast(I32))
+        load_scale_rows(nc.sync, w_sc, w1_scales)
+        n2_sb = load_list("n2_sb", n2)
+        n1_sb = load_list("n1_sb", n1)
+        ga_sb = keep.tile([P, PACK], F32)
+        gb_sb = keep.tile([P, PACK], F32)
+        nc.sync.dma_start(gb_sb[:], gb.rearrange("(p t) o -> p (t o)", t=PACK))
+        nc.sync.dma_start(ga_sb[:], ga.rearrange("(p t) o -> p (t o)", t=PACK))
+        n3_sb = load_list("n3_sb", n3)
+        n4_sb = load_list("n4_sb", n4)
+        n5_sb = load_list("n5_sb", n5)
+        n6_sb = load_list("n6_sb", n6)
+        n8_sb = load_list("n8_sb", n8)
+        n9_sb = load_list("n9_sb", n9)
+        n7_sb = load_list("n7_sb", n7)
+
+        w_wd_dealt = keep.tile([P, 2 * S], U8, align_bytes=64)
+        w_sc_dealt = keep.tile([P, S], U8, align_bytes=64)
+        nc.vector.tensor_copy(
+            out=w_wd_dealt[:].rearrange("p (t m b) -> p t m b", t=PACK, b=2),
+            in_=w_wd[:].rearrange("p (m t b) -> p t m b", t=PACK, b=2),
+        )
+        nc.vector.tensor_copy(
+            out=w_sc_dealt[:].rearrange("p (t m) -> p t m", t=PACK),
+            in_=w_sc[:].rearrange("p (m t) -> p t m", t=PACK),
+        )
+
+        gb34 = keep.tile([P, PACK], F32)
+        nc.scalar.activation(gb34[:], gb_sb[:], ACT.Copy, scale=0.75)
+
+        xq_sc = keep.tile([P, S], U8, align_bytes=64)
+        nc.vector.tensor_copy(xq_sc[:], x_sc[:].indirect(offs_sb[:]))
+        y = [keep.tile([P, S], F32, name="y%d" % t) for t in range(PACK)]
+        for half in range(2):
+            cols = slice(half * W, (half + 1) * W)
+            xq_wd = keep.tile([P, W], U32, align_bytes=64, name="xq_wd%d" % half)
+            nc.vector.tensor_copy(xq_wd[:], x_wd[:].bitcast(U32).indirect(entries(offs_sb, half * W, W)))
+            for pair in range(2):
+                bank = psum.tile([P, 2, W], F32, name="y_ps%d%d" % (half, pair), tag="bank%d" % (2 * half + pair))
+                for u in range(2):
+                    t = 2 * pair + u
+                    nc.tensor.matmul_mx(
+                        out=bank[:, u, :],
+                        lhsT=w_wd_dealt[:, 2 * P * t : 2 * P * (t + 1)].bitcast(FP4X4),
+                        lhsT_scale=w_sc_dealt[:, P * t : P * (t + 1)],
+                        rhs=xq_wd[:].bitcast(FP8X4),
+                        rhs_scale=xq_sc[:, cols],
+                        start=True,
+                        stop=True,
+                    )
+                for u in range(2):
+                    nc.scalar.copy(y[2 * pair + u][:, cols], bank[:, u, :])
+
+        pa = keep.tile([P, PACK, W], F32)
+        pb = keep.tile([P, PACK, W], F32)
+        for t in range(PACK):
+            nc.vector.tensor_copy(pb[:, t, :], y[t][:].indirect(n2_sb[:]))
+            nc.vector.tensor_copy(pa[:, t, :], y[t][:].indirect(n1_sb[:]))
+        pb_abs = keep.tile([P, PACK, W], F32)
+        pb_log = keep.tile([P, PACK, W], F32)
+        inv = keep.tile([P, PACK, W], F32)
+        nc.scalar.activation(pb_abs[:], pb[:], ACT.Abs)
+        nc.scalar.activation(pb_log[:], pb_abs[:], ACT.Ln, bias=0.5)
+        nc.scalar.activation(inv[:], pb_log[:], ACT.Exp, scale=-1.0)
+        rb = keep.tile([P, PACK, W], F32)
+        for pair in range(2):
+            ts = slice(2 * pair, 2 * pair + 2)
+            nc.vector.tensor_tensor(rb[:, ts, :], pa[:, ts, :], pb[:, ts, :], ALU.max)
+        dt = [keep.tile([P, S], F32, name="dt%d" % t) for t in range(PACK)]
+        for t in range(PACK):
+            nc.vector.tensor_copy(dt[t][:].indirect(n2_sb[:]), rb[:, t, :])
+        for t in range(PACK):
+            nc.vector.tensor_tensor(dt[t][:].indirect(n1_sb[:]), pa[:, t, :], inv[:, t, :], ALU.mult)
+
+        yg = [keep.tile([P, S], F32, name="yg%d" % t) for t in range(PACK)]
+        for t in range(PACK):
+            nc.scalar.activation(yg[t][:], y[t][:], ACT.Copy, scale=gb34[:, t : t + 1])
+
+        z = keep.tile([P, PACK, S], F32)
+        for t in range(PACK):
+            nc.scalar.activation(z[:, t, :], dt[t][:], ACT.Copy, scale=ga_sb[:, t : t + 1])
+        z_bf = keep.tile([P, PACK, P, PACK], BF16, align_bytes=64)
+        nc.scalar.activation(
+            z_bf[:].rearrange("p r m t -> p m t r"), z[:].rearrange("p t (m r) -> p m t r", r=PACK), ACT.Copy
+        )
+        z_wd = keep.tile([P, S], U32, align_bytes=64)
+        z_sc = keep.tile([P, S], U8, align_bytes=64)
+
+        s = [keep.tile([P, S], F32, name="s%d" % t) for t in range(PACK)]
+
+        def z2_products(start, count):
+            g3 = keep.tile([P, PACK, count], F32, name="g3_%d" % start)
+            g5 = keep.tile([P, PACK, count], F32, name="g5_%d" % start)
+            p34 = keep.tile([P, PACK, count], F32, name="p34_%d" % start)
+            p56 = keep.tile([P, PACK, count], F32, name="p56_%d" % start)
+            for t in range(PACK):
+                nc.vector.tensor_copy(g3[:, t, :], yg[t][:].indirect(entries(n3_sb, start, count)))
+                nc.vector.tensor_copy(g5[:, t, :], yg[t][:].indirect(entries(n5_sb, start, count)))
+            for t in range(PACK):
+                nc.vector.tensor_tensor(p34[:, t, :], y[t][:].indirect(entries(n4_sb, start, count)), g3[:, t, :], ALU.mult)
+                nc.vector.tensor_tensor(p56[:, t, :], y[t][:].indirect(entries(n6_sb, start, count)), g5[:, t, :], ALU.mult)
+            z2_bf = keep.tile([P, count, PACK], BF16, align_bytes=64, name="z2_bf%d" % start)
+            nc.vector.tensor_tensor(four_lines_packed(z2_bf[:]), four_lines(p34[:]), four_lines(p56[:]), ALU.subtract)
+            return z2_bf
+
+        def s_columns(start, count, z2_bf, banks):
+            z2_wd = keep.tile([P, count], U32, align_bytes=64, name="z2_wd%d" % start)
+            z2_sc = keep.tile([P, count], U8, align_bytes=64, name="z2_sc%d" % start)
+            nc.vector.quantize_mx(
+                out=z2_wd[:].bitcast(FP8X4), scales=z2_sc[:], in_=z2_bf[:].rearrange("p c t -> p (c t)")
+            )
+            for pair in range(2):
+                bank = psum.tile([P, 2, count], F32, name="s_ps%d%d" % (start, pair), tag="bank%d" % banks[pair])
+                for u in range(2):
+                    r = 2 * pair + u
+                    nc.tensor.matmul_mx(
+                        out=bank[:, u, :],
+                        lhsT=z_wd[:, P * r : P * (r + 1)].bitcast(FP8X4),
+                        lhsT_scale=z_sc[:, P * r : P * (r + 1)],
+                        rhs=z2_wd[:].bitcast(FP8X4),
+                        rhs_scale=z2_sc[:],
+                        start=True,
+                        stop=True,
+                    )
+                for u in range(2):
+                    nc.scalar.activation(s[2 * pair + u][:, start : start + count], bank[:, u, :], ACT.Copy, scale=0.0625)
+
+        for c, (start, count) in enumerate(Z2_CHUNKS):
+            z2_bf = z2_products(start, count)
+            if c == 0:
+                nc.vector.quantize_mx(
+                    out=z_wd[:].bitcast(FP8X4), scales=z_sc[:], in_=z_bf[:].rearrange("p r m t -> p (r m t)")
+                )
+            s_columns(start, count, z2_bf, (2 + 2 * c, 3 + 2 * c))
+
+        out_rows = out_0.rearrange("(p t) j -> p t j", t=PACK)
+        out_words = out_1[0].rearrange("p n t -> p (n t)").bitcast(I32)
+        o_sc = keep.tile([P, S], U8, align_bytes=64)
+        for start, count in OUT_CHUNKS:
+            gate = keep.tile([P, PACK, count], F32, name="gate%d" % start)
+            rest = keep.tile([P, PACK, count], F32, name="rest%d" % start)
+            from9 = keep.tile([P, PACK, count], F32, name="from9_%d" % start)
+            from7 = keep.tile([P, PACK, count], F32, name="from7_%d" % start)
+            o = keep.tile([P, PACK, count], F32, name="o%d" % start)
+            for t in range(PACK):
+                nc.scalar.activation(gate[:, t, :], s[t][:].indirect(entries(n8_sb, start, count)), ACT.Sigmoid)
+                nc.scalar.activation(rest[:, t, :], gate[:, t, :], ACT.Identity, scale=-1.0, bias=1.0)
+                nc.vector.tensor_tensor(from9[:, t, :], s[t][:].indirect(entries(n9_sb, start, count)), gate[:, t, :], ALU.mult)
+                nc.vector.tensor_tensor(from7[:, t, :], s[t][:].indirect(entries(n7_sb, start, count)), rest[:, t, :], ALU.mult)
+            nc.vector.tensor_tensor(o[:], from9[:], from7[:], ALU.add)
+            nc.sync.dma_start(out_rows[:, :, start : start + count], o[:])
+            o_bf = keep.tile([P, count, PACK], BF16, align_bytes=64, name="o_bf%d" % start)
+            nc.scalar.activation(four_lines_packed(o_bf[:]), four_lines(o[:]), ACT.Copy)
+            o_wd = keep.tile([P, count], I32, align_bytes=64, name="o_wd%d" % start)
+            nc.vector.quantize_mx(
+                out=o_wd[:].bitcast(FP8X4), scales=o_sc[:, start : start + count], in_=o_bf[:].rearrange("p c t -> p (c t)")
+            )
+            nc.sync.dma_start(out_words[:, start : start + count], o_wd[:])
+        for q in range(4):
+            queue = nc.sync if q % 2 == 0 else nc.scalar
+            queue.dma_start(out_2[0, 4 * q : 4 * q + 4, :].bitcast(I32), o_sc[32 * q : 32 * q + 4, :].bitcast(I32))

@@ -1,6 +1,7 @@
 from contextlib import ExitStack
 
 import concourse.mybir as mybir
+from concourse.masks import make_identity
 
 F32 = mybir.dt.float32
 BF16 = mybir.dt.bfloat16
@@ -20,8 +21,9 @@ S = 512
 W = 256
 FLOPS = 2 * 2 * 512 * 512 * 512
 
-Z2_CHUNKS = ((0, 256), (256, 128), (384, 128))
-OUT_CHUNKS = ((0, 256), (256, 128), (384, 128))
+MAIN = 384
+LAST = S - MAIN
+MAIN_PIECES = ((0, 256), (256, 128))
 
 
 def entries(list_tile, start, count):
@@ -80,147 +82,233 @@ def tile_picked_selfratiodetlerp_none_po_kernel(
         n7_sb = load_list("n7_sb", n7)
 
         w_wd_dealt = keep.tile([P, 2 * S], U8, align_bytes=64)
-        w_sc_dealt = keep.tile([P, S], U8, align_bytes=64)
+        w_sc_first = keep.tile([P, P], U8, align_bytes=64)
+        w_sc_rest = keep.tile([P, PACK - 1, P], U8, align_bytes=64)
+        w_sc_by_tile = w_sc[:].rearrange("p (m t) -> p t m", t=PACK)
         nc.vector.tensor_copy(
             out=w_wd_dealt[:].rearrange("p (t m b) -> p t m b", t=PACK, b=2),
             in_=w_wd[:].rearrange("p (m t b) -> p t m b", t=PACK, b=2),
-        )
-        nc.vector.tensor_copy(
-            out=w_sc_dealt[:].rearrange("p (t m) -> p t m", t=PACK),
-            in_=w_sc[:].rearrange("p (m t) -> p t m", t=PACK),
         )
 
         gb34 = keep.tile([P, PACK], F32)
         nc.scalar.activation(gb34[:], gb_sb[:], ACT.Copy, scale=0.75)
 
+        ident = keep.tile([P, P], F32)
+        make_identity(nc, ident[:])
+
         xq_sc = keep.tile([P, S], U8, align_bytes=64)
+        xq_wd = keep.tile([P, S], U32, align_bytes=64)
         nc.vector.tensor_copy(xq_sc[:], x_sc[:].indirect(offs_sb[:]))
-        y = [keep.tile([P, S], F32, name="y%d" % t) for t in range(PACK)]
         for half in range(2):
-            cols = slice(half * W, (half + 1) * W)
-            xq_wd = keep.tile([P, W], U32, align_bytes=64, name="xq_wd%d" % half)
-            nc.vector.tensor_copy(xq_wd[:], x_wd[:].bitcast(U32).indirect(entries(offs_sb, half * W, W)))
-            for pair in range(2):
-                bank = psum.tile([P, 2, W], F32, name="y_ps%d%d" % (half, pair), tag="bank%d" % (2 * half + pair))
-                for u in range(2):
-                    t = 2 * pair + u
-                    nc.tensor.matmul_mx(
-                        out=bank[:, u, :],
-                        lhsT=w_wd_dealt[:, 2 * P * t : 2 * P * (t + 1)].bitcast(FP4X4),
-                        lhsT_scale=w_sc_dealt[:, P * t : P * (t + 1)],
-                        rhs=xq_wd[:].bitcast(FP8X4),
-                        rhs_scale=xq_sc[:, cols],
-                        start=True,
-                        stop=True,
-                    )
-                for u in range(2):
-                    nc.scalar.copy(y[2 * pair + u][:, cols], bank[:, u, :])
+            nc.vector.tensor_copy(
+                xq_wd[:, half * W : (half + 1) * W], x_wd[:].bitcast(U32).indirect(entries(offs_sb, half * W, W))
+            )
+            if half == 0:
+                nc.vector.tensor_copy(w_sc_first[:], w_sc_by_tile[:, 0, :])
+            else:
+                nc.vector.tensor_copy(w_sc_rest[:], w_sc_by_tile[:, 1:PACK, :])
+        y = [keep.tile([P, S], F32, name="y%d" % t) for t in range(PACK)]
+        y_jobs = [(0, 0, W), (0, W, W)] + [(t, 0, S) for t in range(1, PACK)]
+        for job, (t, start, count) in enumerate(y_jobs):
+            cols = slice(start, start + count)
+            bank = psum.tile([P, count], F32, name="y_ps%d" % job, tag="bank%d" % job)
+            nc.tensor.matmul_mx(
+                out=bank[:],
+                lhsT=w_wd_dealt[:, 2 * P * t : 2 * P * (t + 1)].bitcast(FP4X4),
+                lhsT_scale=w_sc_first[:] if t == 0 else w_sc_rest[:, t - 1, :],
+                rhs=xq_wd[:, cols].bitcast(FP8X4),
+                rhs_scale=xq_sc[:, cols],
+                start=True,
+                stop=True,
+            )
+            nc.scalar.copy(y[t][:, cols], bank[:])
 
         pa = keep.tile([P, PACK, W], F32)
         pb = keep.tile([P, PACK, W], F32)
         for t in range(PACK):
             nc.vector.tensor_copy(pb[:, t, :], y[t][:].indirect(n2_sb[:]))
             nc.vector.tensor_copy(pa[:, t, :], y[t][:].indirect(n1_sb[:]))
+        yg = [keep.tile([P, S], F32, name="yg%d" % t) for t in range(PACK)]
+        yn = [keep.tile([P, S], F32, name="yn%d" % t) for t in range(PACK)]
+        for t in range(PACK):
+            nc.scalar.activation(yg[t][:], y[t][:], ACT.Copy, scale=gb34[:, t : t + 1])
+        for t in range(PACK):
+            nc.scalar.activation(yn[t][:], y[t][:], ACT.Copy, scale=-1.0)
         pb_abs = keep.tile([P, PACK, W], F32)
         pb_log = keep.tile([P, PACK, W], F32)
-        inv = keep.tile([P, PACK, W], F32)
+        inv = keep.tile([P, PACK, W], F32, tag="after_scatters", align_bytes=64)
         nc.scalar.activation(pb_abs[:], pb[:], ACT.Abs)
         nc.scalar.activation(pb_log[:], pb_abs[:], ACT.Ln, bias=0.5)
         nc.scalar.activation(inv[:], pb_log[:], ACT.Exp, scale=-1.0)
+        warm = keep.tile([P, 1], F32)
+        nc.scalar.activation(warm[:], inv[:, 0, 0:1], ACT.Sigmoid)
         rb = keep.tile([P, PACK, W], F32)
-        for pair in range(2):
-            ts = slice(2 * pair, 2 * pair + 2)
-            nc.vector.tensor_tensor(rb[:, ts, :], pa[:, ts, :], pb[:, ts, :], ALU.max)
+
+        g35 = keep.tile([P, 2, PACK, MAIN], F32)
+        p34 = keep.tile([P, PACK, MAIN], F32)
+        p56 = keep.tile([P, PACK, MAIN], F32)
+        for t in range(PACK):
+            nc.vector.tensor_copy(g35[:, 0, t, :], yg[t][:].indirect(entries(n3_sb, 0, MAIN)))
+            if t == 0:
+                nc.vector.tensor_tensor(rb[:], pa[:], pb[:], ALU.max)
+            nc.vector.tensor_copy(g35[:, 1, t, :], yg[t][:].indirect(entries(n5_sb, 0, MAIN)))
+            nc.vector.tensor_tensor(p34[:, t, :], y[t][:].indirect(entries(n4_sb, 0, MAIN)), g35[:, 0, t, :], ALU.mult)
+            nc.vector.tensor_tensor(p56[:, t, :], yn[t][:].indirect(entries(n6_sb, 0, MAIN)), g35[:, 1, t, :], ALU.mult)
+        z2_bf = keep.tile([P, MAIN, PACK], BF16, tag="after_z2", align_bytes=64)
+        blocks = MAIN // P
+        turned = [psum.tile([P, PACK, P], F32, name="turned%d" % c, tag="bank%d" % (5 + c)) for c in range(blocks)]
+        for t in range(PACK):
+            for c in range(blocks):
+                cols = slice(c * P, (c + 1) * P)
+                nc.tensor.matmul(turned[c][:, t, :], p34[:, t, cols], ident[:], start=True, stop=False, is_transpose=True)
+                nc.tensor.matmul(turned[c][:, t, :], p56[:, t, cols], ident[:], start=False, stop=True, is_transpose=True)
+        for c in range(blocks):
+            turned_sb = keep.tile([P, PACK, P], F32, name="turned_sb%d" % c)
+            nc.scalar.copy(turned_sb[:], turned[c][:])
+            back = psum.tile([P, PACK, P], F32, name="back%d" % c, tag="bank%d" % c)
+            for t in range(PACK):
+                nc.tensor.transpose(back[:, t, :], turned_sb[:, t, :], ident[:])
+            nc.scalar.copy(z2_bf[:, c * P : (c + 1) * P, :], back[:].rearrange("p t j -> p j t"))
+
         dt = [keep.tile([P, S], F32, name="dt%d" % t) for t in range(PACK)]
         for t in range(PACK):
             nc.vector.tensor_copy(dt[t][:].indirect(n2_sb[:]), rb[:, t, :])
+        z_pair = keep.tile([P, 2, S], F32)
+        z_bf = keep.tile([P, PACK, P, PACK], BF16, tag="after_z", align_bytes=64)
         for t in range(PACK):
             nc.vector.tensor_tensor(dt[t][:].indirect(n1_sb[:]), pa[:, t, :], inv[:, t, :], ALU.mult)
+            if t < 2:
+                nc.scalar.activation(z_pair[:, t, :], dt[t][:], ACT.Copy, scale=ga_sb[:, t : t + 1])
+            if t == 1:
+                nc.scalar.activation(
+                    z_bf[:].rearrange("p r m t -> p m t r")[:, :, 0:2, :],
+                    z_pair[:].rearrange("p t (m r) -> p m t r", r=PACK),
+                    ACT.Copy,
+                )
+            if t >= 2:
+                nc.scalar.activation(
+                    z_bf[:, :, :, t], dt[t][:].rearrange("p (m r) -> p r m", r=PACK), ACT.Copy, scale=ga_sb[:, t : t + 1]
+                )
 
-        yg = [keep.tile([P, S], F32, name="yg%d" % t) for t in range(PACK)]
-        for t in range(PACK):
-            nc.scalar.activation(yg[t][:], y[t][:], ACT.Copy, scale=gb34[:, t : t + 1])
-
-        z = keep.tile([P, PACK, S], F32)
-        for t in range(PACK):
-            nc.scalar.activation(z[:, t, :], dt[t][:], ACT.Copy, scale=ga_sb[:, t : t + 1])
-        z_bf = keep.tile([P, PACK, P, PACK], BF16, align_bytes=64)
-        nc.scalar.activation(
-            z_bf[:].rearrange("p r m t -> p m t r"), z[:].rearrange("p t (m r) -> p m t r", r=PACK), ACT.Copy
-        )
+        z2_wd = keep.tile([P, S], U32, align_bytes=64)
+        z2_sc = keep.tile([P, S], U8, align_bytes=64)
         z_wd = keep.tile([P, S], U32, align_bytes=64)
         z_sc = keep.tile([P, S], U8, align_bytes=64)
+        s = [keep.tile([P, S], F32, name="s%d" % r) for r in range(PACK)]
 
-        s = [keep.tile([P, S], F32, name="s%d" % t) for t in range(PACK)]
-
-        def z2_products(start, count):
-            g3 = keep.tile([P, PACK, count], F32, name="g3_%d" % start)
-            g5 = keep.tile([P, PACK, count], F32, name="g5_%d" % start)
-            p34 = keep.tile([P, PACK, count], F32, name="p34_%d" % start)
-            p56 = keep.tile([P, PACK, count], F32, name="p56_%d" % start)
-            for t in range(PACK):
-                nc.vector.tensor_copy(g3[:, t, :], yg[t][:].indirect(entries(n3_sb, start, count)))
-                nc.vector.tensor_copy(g5[:, t, :], yg[t][:].indirect(entries(n5_sb, start, count)))
-            for t in range(PACK):
-                nc.vector.tensor_tensor(p34[:, t, :], y[t][:].indirect(entries(n4_sb, start, count)), g3[:, t, :], ALU.mult)
-                nc.vector.tensor_tensor(p56[:, t, :], y[t][:].indirect(entries(n6_sb, start, count)), g5[:, t, :], ALU.mult)
-            z2_bf = keep.tile([P, count, PACK], BF16, align_bytes=64, name="z2_bf%d" % start)
-            nc.vector.tensor_tensor(four_lines_packed(z2_bf[:]), four_lines(p34[:]), four_lines(p56[:]), ALU.subtract)
-            return z2_bf
-
-        def s_columns(start, count, z2_bf, banks):
-            z2_wd = keep.tile([P, count], U32, align_bytes=64, name="z2_wd%d" % start)
-            z2_sc = keep.tile([P, count], U8, align_bytes=64, name="z2_sc%d" % start)
+        def quantize(words, scales, start, count, packed):
+            cols = slice(start, start + count)
             nc.vector.quantize_mx(
-                out=z2_wd[:].bitcast(FP8X4), scales=z2_sc[:], in_=z2_bf[:].rearrange("p c t -> p (c t)")
+                out=words[:, cols].bitcast(FP8X4), scales=scales[:, cols], in_=packed.rearrange("p c t -> p (c t)")
             )
-            for pair in range(2):
-                bank = psum.tile([P, 2, count], F32, name="s_ps%d%d" % (start, pair), tag="bank%d" % banks[pair])
-                for u in range(2):
-                    r = 2 * pair + u
-                    nc.tensor.matmul_mx(
-                        out=bank[:, u, :],
-                        lhsT=z_wd[:, P * r : P * (r + 1)].bitcast(FP8X4),
-                        lhsT_scale=z_sc[:, P * r : P * (r + 1)],
-                        rhs=z2_wd[:].bitcast(FP8X4),
-                        rhs_scale=z2_sc[:],
-                        start=True,
-                        stop=True,
-                    )
-                for u in range(2):
-                    nc.scalar.activation(s[2 * pair + u][:, start : start + count], bank[:, u, :], ACT.Copy, scale=0.0625)
 
-        for c, (start, count) in enumerate(Z2_CHUNKS):
-            z2_bf = z2_products(start, count)
-            if c == 0:
-                nc.vector.quantize_mx(
-                    out=z_wd[:].bitcast(FP8X4), scales=z_sc[:], in_=z_bf[:].rearrange("p r m t -> p (r m t)")
-                )
-            s_columns(start, count, z2_bf, (2 + 2 * c, 3 + 2 * c))
+        def s_product(out, r, start, count):
+            nc.tensor.matmul_mx(
+                out=out,
+                lhsT=z_wd[:, P * r : P * (r + 1)].bitcast(FP8X4),
+                lhsT_scale=z_sc[:, P * r : P * (r + 1)],
+                rhs=z2_wd[:, start : start + count].bitcast(FP8X4),
+                rhs_scale=z2_sc[:, start : start + count],
+                start=True,
+                stop=True,
+            )
+
+        g35_last = keep.tile([P, 2, PACK, LAST], F32, tag="after_scatters", align_bytes=64)
+        for t in range(PACK):
+            nc.vector.tensor_copy(g35_last[:, 0, t, :], yg[t][:].indirect(entries(n3_sb, MAIN, LAST)))
+            nc.vector.tensor_copy(g35_last[:, 1, t, :], yg[t][:].indirect(entries(n5_sb, MAIN, LAST)))
+        for start, count in MAIN_PIECES:
+            quantize(z2_wd, z2_sc, start, count, z2_bf[:, start : start + count, :])
+        p34_last = keep.tile([P, PACK, LAST], F32, tag="after_z2", align_bytes=64)
+        for t in range(PACK):
+            nc.vector.tensor_tensor(
+                p34_last[:, t, :], y[t][:].indirect(entries(n4_sb, MAIN, LAST)), g35_last[:, 0, t, :], ALU.mult
+            )
+        quantize(z_wd, z_sc, 0, S, z_bf[:].rearrange("p r m t -> p (r m) t"))
+        for r in range(PACK):
+            bank = psum.tile([P, MAIN], F32, name="s_main%d" % r, tag="bank%d" % (4 + r))
+            for start, count in MAIN_PIECES:
+                s_product(bank[:, start : start + count], r, start, count)
+            nc.scalar.activation(s[r][:, 0:MAIN], bank[:], ACT.Copy, scale=0.0625)
+        p56_last = keep.tile([P, PACK, LAST], F32, tag="after_z", align_bytes=64)
+        for t in range(PACK):
+            nc.vector.tensor_tensor(
+                p56_last[:, t, :], yn[t][:].indirect(entries(n6_sb, MAIN, LAST)), g35_last[:, 1, t, :], ALU.mult
+            )
+        z2_bf_last = keep.tile([P, LAST, PACK], BF16, align_bytes=64)
+        nc.vector.tensor_tensor(four_lines_packed(z2_bf_last[:]), four_lines(p34_last[:]), four_lines(p56_last[:]), ALU.add)
+        quantize(z2_wd, z2_sc, MAIN, LAST, z2_bf_last[:])
+        for r in range(PACK):
+            bank = psum.tile([P, LAST], F32, name="s_last%d" % r, tag="bank%d" % r)
+            s_product(bank[:], r, MAIN, LAST)
+            nc.scalar.activation(s[r][:, MAIN:S], bank[:], ACT.Copy, scale=0.0625)
 
         out_rows = out_0.rearrange("(p t) j -> p t j", t=PACK)
         out_words = out_1[0].rearrange("p n t -> p (n t)").bitcast(I32)
+        o_wd = keep.tile([P, S], I32, align_bytes=64)
         o_sc = keep.tile([P, S], U8, align_bytes=64)
-        for start, count in OUT_CHUNKS:
-            gate = keep.tile([P, PACK, count], F32, name="gate%d" % start)
-            rest = keep.tile([P, PACK, count], F32, name="rest%d" % start)
-            from9 = keep.tile([P, PACK, count], F32, name="from9_%d" % start)
-            from7 = keep.tile([P, PACK, count], F32, name="from7_%d" % start)
-            o = keep.tile([P, PACK, count], F32, name="o%d" % start)
-            for t in range(PACK):
-                nc.scalar.activation(gate[:, t, :], s[t][:].indirect(entries(n8_sb, start, count)), ACT.Sigmoid)
+        gate = keep.tile([P, PACK, MAIN], F32)
+        rest = keep.tile([P, PACK, MAIN], F32)
+        gate_last = keep.tile([P, PACK, LAST], F32)
+        rest_last = keep.tile([P, PACK, LAST], F32)
+        for t in range(PACK):
+            for start, count in MAIN_PIECES:
+                nc.scalar.activation(
+                    gate[:, t, start : start + count], s[t][:].indirect(entries(n8_sb, start, count)), ACT.Sigmoid
+                )
+            if t > 0:
                 nc.scalar.activation(rest[:, t, :], gate[:, t, :], ACT.Identity, scale=-1.0, bias=1.0)
-                nc.vector.tensor_tensor(from9[:, t, :], s[t][:].indirect(entries(n9_sb, start, count)), gate[:, t, :], ALU.mult)
-                nc.vector.tensor_tensor(from7[:, t, :], s[t][:].indirect(entries(n7_sb, start, count)), rest[:, t, :], ALU.mult)
-            nc.vector.tensor_tensor(o[:], from9[:], from7[:], ALU.add)
-            nc.sync.dma_start(out_rows[:, :, start : start + count], o[:])
-            o_bf = keep.tile([P, count, PACK], BF16, align_bytes=64, name="o_bf%d" % start)
-            nc.scalar.activation(four_lines_packed(o_bf[:]), four_lines(o[:]), ACT.Copy)
-            o_wd = keep.tile([P, count], I32, align_bytes=64, name="o_wd%d" % start)
-            nc.vector.quantize_mx(
-                out=o_wd[:].bitcast(FP8X4), scales=o_sc[:, start : start + count], in_=o_bf[:].rearrange("p c t -> p (c t)")
+        for t in range(PACK):
+            nc.scalar.activation(gate_last[:, t, :], s[t][:].indirect(entries(n8_sb, MAIN, LAST)), ACT.Sigmoid)
+        nc.scalar.activation(rest_last[:], gate_last[:], ACT.Identity, scale=-1.0, bias=1.0)
+
+        from9 = keep.tile([P, PACK, MAIN], F32)
+        from7 = keep.tile([P, PACK, MAIN], F32)
+        o = keep.tile([P, PACK, MAIN], F32)
+        for start, count in MAIN_PIECES:
+            nc.vector.tensor_copy(from7[:, 0, start : start + count], s[0][:].indirect(entries(n7_sb, start, count)))
+        for start, count in MAIN_PIECES:
+            cols = slice(start, start + count)
+            nc.vector.tensor_tensor(
+                rest[:, 0, cols], s[0][:].indirect(entries(n9_sb, start, count)), from7[:, 0, cols], ALU.subtract
             )
-            nc.sync.dma_start(out_words[:, start : start + count], o_wd[:])
+        for t in range(1, PACK):
+            nc.vector.tensor_tensor(from9[:, t, :], s[t][:].indirect(entries(n9_sb, 0, MAIN)), gate[:, t, :], ALU.mult)
+            if t == 1:
+                nc.vector.tensor_tensor(from9[:, 0, :], rest[:, 0, :], gate[:, 0, :], ALU.mult)
+            if t == PACK - 1:
+                nc.vector.tensor_tensor(o[:, 0:t, :], from9[:, 0:t, :], from7[:, 0:t, :], ALU.add)
+            nc.vector.tensor_tensor(from7[:, t, :], s[t][:].indirect(entries(n7_sb, 0, MAIN)), rest[:, t, :], ALU.mult)
+
+        from9_last = keep.tile([P, PACK, LAST], F32)
+        from7_last = keep.tile([P, PACK, LAST], F32)
+        o_last = keep.tile([P, PACK, LAST], F32)
+        o_bf = keep.tile([P, MAIN, PACK], BF16, tag="after_o", align_bytes=64)
+        for t in range(PACK):
+            nc.vector.tensor_tensor(
+                from9_last[:, t, :], s[t][:].indirect(entries(n9_sb, MAIN, LAST)), gate_last[:, t, :], ALU.mult
+            )
+            if t == 0:
+                nc.vector.tensor_tensor(o[:, PACK - 1, :], from9[:, PACK - 1, :], from7[:, PACK - 1, :], ALU.add)
+                nc.sync.dma_start(out_rows[:, :, 0:MAIN], o[:])
+                for start, count in MAIN_PIECES:
+                    cols = slice(start, start + count)
+                    nc.scalar.activation(four_lines_packed(o_bf[:, cols, :]), four_lines(o[:, :, cols]), ACT.Copy)
+            nc.vector.tensor_tensor(
+                from7_last[:, t, :], s[t][:].indirect(entries(n7_sb, MAIN, LAST)), rest_last[:, t, :], ALU.mult
+            )
+        for start, count in MAIN_PIECES:
+            quantize(o_wd, o_sc, start, count, o_bf[:, start : start + count, :])
+        nc.sync.dma_start(out_words[:, 0:MAIN], o_wd[:, 0:MAIN])
+        t = PACK - 1
+        nc.vector.tensor_tensor(o_last[:, 0:t, :], from9_last[:, 0:t, :], from7_last[:, 0:t, :], ALU.add)
+        nc.sync.dma_start(out_rows[:, 0:t, MAIN:S], o_last[:, 0:t, :])
+        o_bf_last = keep.tile([P, LAST, PACK], BF16, tag="after_o", align_bytes=64)
+        nc.vector.tensor_tensor(four_lines_packed(o_bf_last[:]), four_lines(from9_last[:]), four_lines(from7_last[:]), ALU.add)
+        nc.vector.tensor_tensor(o_last[:, t, :], from9_last[:, t, :], from7_last[:, t, :], ALU.add)
+        nc.scalar.dma_start(out_rows[:, t, MAIN:S], o_last[:, t, :])
+        quantize(o_wd, o_sc, MAIN, LAST, o_bf_last[:])
+        nc.sync.dma_start(out_words[:, MAIN:S], o_wd[:, MAIN:S])
         for q in range(4):
             queue = nc.sync if q % 2 == 0 else nc.scalar
             queue.dma_start(out_2[0, 4 * q : 4 * q + 4, :].bitcast(I32), o_sc[32 * q : 32 * q + 4, :].bitcast(I32))

@@ -1,7 +1,6 @@
 from contextlib import ExitStack
 
 import concourse.mybir as mybir
-from concourse.masks import make_identity
 
 F32 = mybir.dt.float32
 BF16 = mybir.dt.bfloat16
@@ -93,8 +92,6 @@ def tile_picked_selfratiodetlerp_none_po_kernel(
         gb34 = keep.tile([P, PACK], F32)
         nc.scalar.activation(gb34[:], gb_sb[:], ACT.Copy, scale=0.75)
 
-        ident = keep.tile([P, P], F32)
-        make_identity(nc, ident[:])
 
         xq_sc = keep.tile([P, S], U8, align_bytes=64)
         xq_wd = keep.tile([P, S], U32, align_bytes=64)
@@ -129,11 +126,8 @@ def tile_picked_selfratiodetlerp_none_po_kernel(
             nc.vector.tensor_copy(pb[:, t, :], y[t][:].indirect(n2_sb[:]))
             nc.vector.tensor_copy(pa[:, t, :], y[t][:].indirect(n1_sb[:]))
         yg = [keep.tile([P, S], F32, name="yg%d" % t) for t in range(PACK)]
-        yn = [keep.tile([P, S], F32, name="yn%d" % t) for t in range(PACK)]
         for t in range(PACK):
             nc.scalar.activation(yg[t][:], y[t][:], ACT.Copy, scale=gb34[:, t : t + 1])
-        for t in range(PACK):
-            nc.scalar.activation(yn[t][:], y[t][:], ACT.Copy, scale=-1.0)
         pb_abs = keep.tile([P, PACK, W], F32)
         pb_log = keep.tile([P, PACK, W], F32)
         inv = keep.tile([P, PACK, W], F32, tag="after_scatters", align_bytes=64)
@@ -144,33 +138,24 @@ def tile_picked_selfratiodetlerp_none_po_kernel(
         nc.scalar.activation(warm[:], inv[:, 0, 0:1], ACT.Sigmoid)
         rb = keep.tile([P, PACK, W], F32)
 
-        g35 = keep.tile([P, 2, PACK, MAIN], F32)
+        z2_bf = keep.tile([P, MAIN, PACK], BF16, tag="after_z2", align_bytes=64)
+        diff = keep.tile([P, PACK, MAIN], F32)
         p34 = keep.tile([P, PACK, MAIN], F32)
         p56 = keep.tile([P, PACK, MAIN], F32)
         for t in range(PACK):
-            nc.vector.tensor_copy(g35[:, 0, t, :], yg[t][:].indirect(entries(n3_sb, 0, MAIN)))
-            if t == 0:
-                nc.vector.tensor_tensor(rb[:], pa[:], pb[:], ALU.max)
-            nc.vector.tensor_copy(g35[:, 1, t, :], yg[t][:].indirect(entries(n5_sb, 0, MAIN)))
-            nc.vector.tensor_tensor(p34[:, t, :], y[t][:].indirect(entries(n4_sb, 0, MAIN)), g35[:, 0, t, :], ALU.mult)
-            nc.vector.tensor_tensor(p56[:, t, :], yn[t][:].indirect(entries(n6_sb, 0, MAIN)), g35[:, 1, t, :], ALU.mult)
-        z2_bf = keep.tile([P, MAIN, PACK], BF16, tag="after_z2", align_bytes=64)
-        blocks = MAIN // P
-        turned = [psum.tile([P, PACK, P], F32, name="turned%d" % c, tag="bank%d" % (5 + c)) for c in range(blocks)]
-        for t in range(PACK):
-            for c in range(blocks):
-                cols = slice(c * P, (c + 1) * P)
-                nc.tensor.matmul(turned[c][:, t, :], p34[:, t, cols], ident[:], start=True, stop=False, is_transpose=True)
-                nc.tensor.matmul(turned[c][:, t, :], p56[:, t, cols], ident[:], start=False, stop=True, is_transpose=True)
-        for c in range(blocks):
-            turned_sb = keep.tile([P, PACK, P], F32, name="turned_sb%d" % c)
-            nc.scalar.copy(turned_sb[:], turned[c][:])
-            back = psum.tile([P, PACK, P], F32, name="back%d" % c, tag="bank%d" % c)
-            for t in range(PACK):
-                nc.tensor.transpose(back[:, t, :], turned_sb[:, t, :], ident[:])
-            nc.scalar.copy(z2_bf[:, c * P : (c + 1) * P, :], back[:].rearrange("p t j -> p j t"))
+            got = []
+            for name, window, list_tile in (("g3", y, n3_sb), ("g4", y, n4_sb), ("g5", y, n5_sb), ("g6", y, n6_sb)):
+                g = keep.tile([P, MAIN], F32, name="%s_%d" % (name, t), tag="held%d_%d" % (len(got), t))
+                nc.vector.tensor_copy(g[:], window[t][:].indirect(entries(list_tile, 0, MAIN)))
+                if t == 0 and not got:
+                    nc.vector.tensor_tensor(rb[:], pa[:], pb[:], ALU.max)
+                got.append(g)
+            nc.gpsimd.tensor_tensor(p34[:, t, :], got[0][:], got[1][:], ALU.mult)
+            nc.gpsimd.tensor_tensor(p56[:, t, :], got[2][:], got[3][:], ALU.mult)
+            nc.gpsimd.tensor_tensor(diff[:, t, :], p34[:, t, :], p56[:, t, :], ALU.subtract)
+            nc.scalar.activation(z2_bf[:, :, t], diff[:, t, :], ACT.Copy, scale=gb34[:, t : t + 1])
 
-        dt = [keep.tile([P, S], F32, name="dt%d" % t) for t in range(PACK)]
+        dt = [keep.tile([P, S], F32, name="dt%d" % t, tag="held%d_2" % t) for t in range(PACK)]
         for t in range(PACK):
             nc.vector.tensor_copy(dt[t][:].indirect(n2_sb[:]), rb[:, t, :])
         z_pair = keep.tile([P, 2, S], F32)
@@ -233,10 +218,10 @@ def tile_picked_selfratiodetlerp_none_po_kernel(
         p56_last = keep.tile([P, PACK, LAST], F32, tag="after_z", align_bytes=64)
         for t in range(PACK):
             nc.vector.tensor_tensor(
-                p56_last[:, t, :], yn[t][:].indirect(entries(n6_sb, MAIN, LAST)), g35_last[:, 1, t, :], ALU.mult
+                p56_last[:, t, :], y[t][:].indirect(entries(n6_sb, MAIN, LAST)), g35_last[:, 1, t, :], ALU.mult
             )
         z2_bf_last = keep.tile([P, LAST, PACK], BF16, align_bytes=64)
-        nc.vector.tensor_tensor(four_lines_packed(z2_bf_last[:]), four_lines(p34_last[:]), four_lines(p56_last[:]), ALU.add)
+        nc.vector.tensor_tensor(four_lines_packed(z2_bf_last[:]), four_lines(p34_last[:]), four_lines(p56_last[:]), ALU.subtract)
         quantize(z2_wd, z2_sc, MAIN, LAST, z2_bf_last[:])
         for r in range(PACK):
             bank = psum.tile([P, LAST], F32, name="s_last%d" % r, tag="bank%d" % r)

from contextlib import ExitStack

import concourse.mybir as mybir

F32 = mybir.dt.float32
BF16 = mybir.dt.bfloat16
I32 = mybir.dt.int32
U32 = mybir.dt.uint32
U16 = mybir.dt.uint16
U8 = mybir.dt.uint8
FP8X4 = mybir.dt.float8_e4m3fn_x4
FP4X4 = mybir.dt.float4_e2m1fn_x4
ALU = mybir.AluOpType
ACT = mybir.ActivationFunctionType

P = 128
PACK = 4
T = 2048
S = 512
W = 256
FLOPS = 2 * 2 * 512 * 512 * 512

MAIN = 384
LAST = S - MAIN
MAIN_PIECES = ((0, 256), (256, 128))


def entries(list_tile, start, count):
    return list_tile[:, start // 16 : (start + count) // 16]


def four_lines(ap_tc):
    return ap_tc.rearrange("p t (c i) -> p c t i", i=4)


def four_lines_packed(ap_ct):
    return ap_ct.rearrange("p (c i) t -> p c t i", i=4)


def tile_picked_selfratiodetlerp_none_po_kernel(
    tc, x_words, x_scales, w1_words, w1_scales, ga, gb, offs, n1, n2, n3, n4, n5, n6, n7, n8, n9, out_0, out_1, out_2
):
    nc = tc.nc
    with ExitStack() as ctx:
        lists = ctx.enter_context(tc.tile_pool(name="lists", bufs=1))
        keep = ctx.enter_context(tc.tile_pool(name="keep", bufs=1))
        psum = ctx.enter_context(tc.psum_pool(name="psum", bufs=1))

        def load_list(name, src):
            tile = lists.tile([P, src.shape[1]], U16, name=name)
            nc.sync.dma_start(tile[:], src)
            return tile

        def load_scale_rows(queue, tile, src):
            for q in range(4):
                rows = src[0, 4 * q : 4 * q + 4, :].bitcast(I32)
                queue.dma_start(tile[32 * q : 32 * q + 32, :].bitcast(I32), rows.partition_broadcast(8))

        x_sc = keep.tile([P, T], U8, align_bytes=64)
        w_sc = keep.tile([P, S], U8, align_bytes=64)

        x_wd = keep.tile([P, T], I32, align_bytes=64)
        w_wd = keep.tile([P, 2 * S], U8, align_bytes=64)
        offs_sb = load_list("offs_sb", offs)
        load_scale_rows(nc.sync, x_sc, x_scales)
        nc.sync.dma_start(w_wd[:].bitcast(I32), w1_words[0].bitcast(I32))
        nc.sync.dma_start(x_wd[:], x_words[0].rearrange("p n t -> p (n t)").bitcast(I32))
        load_scale_rows(nc.sync, w_sc, w1_scales)
        n2_sb = load_list("n2_sb", n2)
        n1_sb = load_list("n1_sb", n1)
        ga_sb = keep.tile([P, PACK], F32)
        gb_sb = keep.tile([P, PACK], F32)
        nc.sync.dma_start(gb_sb[:], gb.rearrange("(p t) o -> p (t o)", t=PACK))
        nc.sync.dma_start(ga_sb[:], ga.rearrange("(p t) o -> p (t o)", t=PACK))
        n3_sb = load_list("n3_sb", n3)
        n4_sb = load_list("n4_sb", n4)
        n5_sb = load_list("n5_sb", n5)
        n6_sb = load_list("n6_sb", n6)
        n8_sb = load_list("n8_sb", n8)
        n9_sb = load_list("n9_sb", n9)
        n7_sb = load_list("n7_sb", n7)

        w_wd_dealt = keep.tile([P, 2 * S], U8, align_bytes=64)
        w_sc_first = keep.tile([P, P], U8, align_bytes=64)
        w_sc_rest = keep.tile([P, PACK - 1, P], U8, align_bytes=64)
        w_sc_by_tile = w_sc[:].rearrange("p (m t) -> p t m", t=PACK)
        nc.vector.tensor_copy(
            out=w_wd_dealt[:].rearrange("p (t m b) -> p t m b", t=PACK, b=2),
            in_=w_wd[:].rearrange("p (m t b) -> p t m b", t=PACK, b=2),
        )

        gb34 = keep.tile([P, PACK], F32)
        nc.scalar.activation(gb34[:], gb_sb[:], ACT.Copy, scale=0.75)


        xq_sc = keep.tile([P, S], U8, align_bytes=64)
        xq_wd = keep.tile([P, S], U32, align_bytes=64)
        nc.vector.tensor_copy(xq_sc[:], x_sc[:].indirect(offs_sb[:]))
        for half in range(2):
            nc.vector.tensor_copy(
                xq_wd[:, half * W : (half + 1) * W], x_wd[:].bitcast(U32).indirect(entries(offs_sb, half * W, W))
            )
            if half == 0:
                nc.vector.tensor_copy(w_sc_first[:], w_sc_by_tile[:, 0, :])
            else:
                nc.vector.tensor_copy(w_sc_rest[:], w_sc_by_tile[:, 1:PACK, :])
        y = [keep.tile([P, S], F32, name="y%d" % t) for t in range(PACK)]
        y_jobs = [(0, 0, W), (0, W, W)] + [(t, 0, S) for t in range(1, PACK)]
        for job, (t, start, count) in enumerate(y_jobs):
            cols = slice(start, start + count)
            bank = psum.tile([P, count], F32, name="y_ps%d" % job, tag="bank%d" % job)
            nc.tensor.matmul_mx(
                out=bank[:],
                lhsT=w_wd_dealt[:, 2 * P * t : 2 * P * (t + 1)].bitcast(FP4X4),
                lhsT_scale=w_sc_first[:] if t == 0 else w_sc_rest[:, t - 1, :],
                rhs=xq_wd[:, cols].bitcast(FP8X4),
                rhs_scale=xq_sc[:, cols],
                start=True,
                stop=True,
            )
            nc.scalar.copy(y[t][:, cols], bank[:])

        pa = keep.tile([P, PACK, W], F32)
        pb = keep.tile([P, PACK, W], F32)
        for t in range(PACK):
            nc.vector.tensor_copy(pb[:, t, :], y[t][:].indirect(n2_sb[:]))
            nc.vector.tensor_copy(pa[:, t, :], y[t][:].indirect(n1_sb[:]))
        yg = [keep.tile([P, S], F32, name="yg%d" % t) for t in range(PACK)]
        for t in range(PACK):
            nc.scalar.activation(yg[t][:], y[t][:], ACT.Copy, scale=gb34[:, t : t + 1])
        pb_abs = keep.tile([P, PACK, W], F32)
        pb_log = keep.tile([P, PACK, W], F32)
        inv = keep.tile([P, PACK, W], F32, tag="after_scatters", align_bytes=64)
        nc.scalar.activation(pb_abs[:], pb[:], ACT.Abs)
        nc.scalar.activation(pb_log[:], pb_abs[:], ACT.Ln, bias=0.5)
        nc.scalar.activation(inv[:], pb_log[:], ACT.Exp, scale=-1.0)
        warm = keep.tile([P, 1], F32)
        nc.scalar.activation(warm[:], inv[:, 0, 0:1], ACT.Sigmoid)
        rb = keep.tile([P, PACK, W], F32)

        z2_bf = keep.tile([P, MAIN, PACK], BF16, tag="after_z2", align_bytes=64)
        diff = keep.tile([P, PACK, MAIN], F32)
        p34 = keep.tile([P, PACK, MAIN], F32)
        p56 = keep.tile([P, PACK, MAIN], F32)
        for t in range(PACK):
            got = []
            for name, window, list_tile in (("g3", y, n3_sb), ("g4", y, n4_sb), ("g5", y, n5_sb), ("g6", y, n6_sb)):
                g = keep.tile([P, MAIN], F32, name="%s_%d" % (name, t), tag="held%d_%d" % (len(got), t))
                nc.vector.tensor_copy(g[:], window[t][:].indirect(entries(list_tile, 0, MAIN)))
                if t == 0 and not got:
                    nc.vector.tensor_tensor(rb[:], pa[:], pb[:], ALU.max)
                got.append(g)
            nc.gpsimd.tensor_tensor(p34[:, t, :], got[0][:], got[1][:], ALU.mult)
            nc.gpsimd.tensor_tensor(p56[:, t, :], got[2][:], got[3][:], ALU.mult)
            nc.gpsimd.tensor_tensor(diff[:, t, :], p34[:, t, :], p56[:, t, :], ALU.subtract)
            nc.scalar.activation(z2_bf[:, :, t], diff[:, t, :], ACT.Copy, scale=gb34[:, t : t + 1])

        dt = [keep.tile([P, S], F32, name="dt%d" % t, tag="held%d_2" % t) for t in range(PACK)]
        for t in range(PACK):
            nc.vector.tensor_copy(dt[t][:].indirect(n2_sb[:]), rb[:, t, :])
        z_pair = keep.tile([P, 2, S], F32)
        z_bf = keep.tile([P, PACK, P, PACK], BF16, tag="after_z", align_bytes=64)
        for t in range(PACK):
            nc.vector.tensor_tensor(dt[t][:].indirect(n1_sb[:]), pa[:, t, :], inv[:, t, :], ALU.mult)
            if t < 2:
                nc.scalar.activation(z_pair[:, t, :], dt[t][:], ACT.Copy, scale=ga_sb[:, t : t + 1])
            if t == 1:
                nc.scalar.activation(
                    z_bf[:].rearrange("p r m t -> p m t r")[:, :, 0:2, :],
                    z_pair[:].rearrange("p t (m r) -> p m t r", r=PACK),
                    ACT.Copy,
                )
            if t >= 2:
                nc.scalar.activation(
                    z_bf[:, :, :, t], dt[t][:].rearrange("p (m r) -> p r m", r=PACK), ACT.Copy, scale=ga_sb[:, t : t + 1]
                )

        z2_wd = keep.tile([P, S], U32, align_bytes=64)
        z2_sc = keep.tile([P, S], U8, align_bytes=64)
        z_wd = keep.tile([P, S], U32, align_bytes=64)
        z_sc = keep.tile([P, S], U8, align_bytes=64)
        s = [keep.tile([P, S], F32, name="s%d" % r) for r in range(PACK)]

        def quantize(words, scales, start, count, packed):
            cols = slice(start, start + count)
            nc.vector.quantize_mx(
                out=words[:, cols].bitcast(FP8X4), scales=scales[:, cols], in_=packed.rearrange("p c t -> p (c t)")
            )

        def s_product(out, r, start, count):
            nc.tensor.matmul_mx(
                out=out,
                lhsT=z_wd[:, P * r : P * (r + 1)].bitcast(FP8X4),
                lhsT_scale=z_sc[:, P * r : P * (r + 1)],
                rhs=z2_wd[:, start : start + count].bitcast(FP8X4),
                rhs_scale=z2_sc[:, start : start + count],
                start=True,
                stop=True,
            )

        g35_last = keep.tile([P, 2, PACK, LAST], F32, tag="after_scatters", align_bytes=64)
        for t in range(PACK):
            nc.vector.tensor_copy(g35_last[:, 0, t, :], yg[t][:].indirect(entries(n3_sb, MAIN, LAST)))
            nc.vector.tensor_copy(g35_last[:, 1, t, :], yg[t][:].indirect(entries(n5_sb, MAIN, LAST)))
        for start, count in MAIN_PIECES:
            quantize(z2_wd, z2_sc, start, count, z2_bf[:, start : start + count, :])
        p34_last = keep.tile([P, PACK, LAST], F32, tag="after_z2", align_bytes=64)
        for t in range(PACK):
            nc.vector.tensor_tensor(
                p34_last[:, t, :], y[t][:].indirect(entries(n4_sb, MAIN, LAST)), g35_last[:, 0, t, :], ALU.mult
            )
        quantize(z_wd, z_sc, 0, S, z_bf[:].rearrange("p r m t -> p (r m) t"))
        for r in range(PACK):
            bank = psum.tile([P, MAIN], F32, name="s_main%d" % r, tag="bank%d" % (4 + r))
            for start, count in MAIN_PIECES:
                s_product(bank[:, start : start + count], r, start, count)
            nc.scalar.activation(s[r][:, 0:MAIN], bank[:], ACT.Copy, scale=0.0625)
        p56_last = keep.tile([P, PACK, LAST], F32, tag="after_z", align_bytes=64)
        for t in range(PACK):
            nc.vector.tensor_tensor(
                p56_last[:, t, :], y[t][:].indirect(entries(n6_sb, MAIN, LAST)), g35_last[:, 1, t, :], ALU.mult
            )
        z2_bf_last = keep.tile([P, LAST, PACK], BF16, align_bytes=64)
        nc.vector.tensor_tensor(four_lines_packed(z2_bf_last[:]), four_lines(p34_last[:]), four_lines(p56_last[:]), ALU.subtract)
        quantize(z2_wd, z2_sc, MAIN, LAST, z2_bf_last[:])
        for r in range(PACK):
            bank = psum.tile([P, LAST], F32, name="s_last%d" % r, tag="bank%d" % r)
            s_product(bank[:], r, MAIN, LAST)
            nc.scalar.activation(s[r][:, MAIN:S], bank[:], ACT.Copy, scale=0.0625)

        out_rows = out_0.rearrange("(p t) j -> p t j", t=PACK)
        out_words = out_1[0].rearrange("p n t -> p (n t)").bitcast(I32)
        o_wd = keep.tile([P, S], I32, align_bytes=64)
        o_sc = keep.tile([P, S], U8, align_bytes=64)
        gate = keep.tile([P, PACK, MAIN], F32)
        rest = keep.tile([P, PACK, MAIN], F32)
        gate_last = keep.tile([P, PACK, LAST], F32)
        rest_last = keep.tile([P, PACK, LAST], F32)
        for t in range(PACK):
            for start, count in MAIN_PIECES:
                nc.scalar.activation(
                    gate[:, t, start : start + count], s[t][:].indirect(entries(n8_sb, start, count)), ACT.Sigmoid
                )
            if t > 0:
                nc.scalar.activation(rest[:, t, :], gate[:, t, :], ACT.Identity, scale=-1.0, bias=1.0)
        for t in range(PACK):
            nc.scalar.activation(gate_last[:, t, :], s[t][:].indirect(entries(n8_sb, MAIN, LAST)), ACT.Sigmoid)
        nc.scalar.activation(rest_last[:], gate_last[:], ACT.Identity, scale=-1.0, bias=1.0)

        from9 = keep.tile([P, PACK, MAIN], F32)
        from7 = keep.tile([P, PACK, MAIN], F32)
        o = keep.tile([P, PACK, MAIN], F32)
        for start, count in MAIN_PIECES:
            nc.vector.tensor_copy(from7[:, 0, start : start + count], s[0][:].indirect(entries(n7_sb, start, count)))
        for start, count in MAIN_PIECES:
            cols = slice(start, start + count)
            nc.vector.tensor_tensor(
                rest[:, 0, cols], s[0][:].indirect(entries(n9_sb, start, count)), from7[:, 0, cols], ALU.subtract
            )
        for t in range(1, PACK):
            nc.vector.tensor_tensor(from9[:, t, :], s[t][:].indirect(entries(n9_sb, 0, MAIN)), gate[:, t, :], ALU.mult)
            if t == 1:
                nc.vector.tensor_tensor(from9[:, 0, :], rest[:, 0, :], gate[:, 0, :], ALU.mult)
            if t == PACK - 1:
                nc.vector.tensor_tensor(o[:, 0:t, :], from9[:, 0:t, :], from7[:, 0:t, :], ALU.add)
            nc.vector.tensor_tensor(from7[:, t, :], s[t][:].indirect(entries(n7_sb, 0, MAIN)), rest[:, t, :], ALU.mult)

        from9_last = keep.tile([P, PACK, LAST], F32)
        from7_last = keep.tile([P, PACK, LAST], F32)
        o_last = keep.tile([P, PACK, LAST], F32)
        o_bf = keep.tile([P, MAIN, PACK], BF16, tag="after_o", align_bytes=64)
        for t in range(PACK):
            nc.vector.tensor_tensor(
                from9_last[:, t, :], s[t][:].indirect(entries(n9_sb, MAIN, LAST)), gate_last[:, t, :], ALU.mult
            )
            if t == 0:
                nc.vector.tensor_tensor(o[:, PACK - 1, :], from9[:, PACK - 1, :], from7[:, PACK - 1, :], ALU.add)
                nc.sync.dma_start(out_rows[:, :, 0:MAIN], o[:])
                for start, count in MAIN_PIECES:
                    cols = slice(start, start + count)
                    nc.scalar.activation(four_lines_packed(o_bf[:, cols, :]), four_lines(o[:, :, cols]), ACT.Copy)
            nc.vector.tensor_tensor(
                from7_last[:, t, :], s[t][:].indirect(entries(n7_sb, MAIN, LAST)), rest_last[:, t, :], ALU.mult
            )
        for start, count in MAIN_PIECES:
            quantize(o_wd, o_sc, start, count, o_bf[:, start : start + count, :])
        nc.sync.dma_start(out_words[:, 0:MAIN], o_wd[:, 0:MAIN])
        t = PACK - 1
        nc.vector.tensor_tensor(o_last[:, 0:t, :], from9_last[:, 0:t, :], from7_last[:, 0:t, :], ALU.add)
        nc.sync.dma_start(out_rows[:, 0:t, MAIN:S], o_last[:, 0:t, :])
        o_bf_last = keep.tile([P, LAST, PACK], BF16, tag="after_o", align_bytes=64)
        nc.vector.tensor_tensor(four_lines_packed(o_bf_last[:]), four_lines(from9_last[:]), four_lines(from7_last[:]), ALU.add)
        nc.vector.tensor_tensor(o_last[:, t, :], from9_last[:, t, :], from7_last[:, t, :], ALU.add)
        nc.scalar.dma_start(out_rows[:, t, MAIN:S], o_last[:, t, :])
        quantize(o_wd, o_sc, MAIN, LAST, o_bf_last[:])
        nc.sync.dma_start(out_words[:, MAIN:S], o_wd[:, MAIN:S])
        for q in range(4):
            queue = nc.sync if q % 2 == 0 else nc.scalar
            queue.dma_start(out_2[0, 4 * q : 4 * q + 4, :].bitcast(I32), o_sc[32 * q : 32 * q + 4, :].bitcast(I32))
